import numpy as np
import ml_dtypes

BF16 = ml_dtypes.bfloat16


def bf(x):
    return np.asarray(x, np.float32).astype(BF16)


def f32(x):
    return np.asarray(x, np.float32)


def f64(x):
    return np.asarray(x).astype(np.float64)


def striped(idx):
    return np.tile(idx.reshape(-1, 16).T, (8, 1))


S, K, M, N, E, Q = 256, 256, 128, 512, 4, 128


def two_experts():
    first = np.random.permutation(S).reshape(E, S // E)
    return np.concatenate([np.random.permutation(np.concatenate([first[e], first[(e + 1) % E]])) for e in range(E)])


def setup_inputs():
    return {"table": bf(np.random.standard_normal((K, S))), "w": bf(np.random.standard_normal((E, K, M)) / np.sqrt(K)), "c": f32(0.2 + 0.8 * np.random.random_sample((1, N))), "offs": striped(two_experts())}


def reference(table, w, c, offs):
    idx = offs[:16].T.reshape(-1)
    x = f64(table)[:, idx]
    y = np.concatenate([f64(w)[e].T @ x[:, e * Q : (e + 1) * Q] for e in range(E)], axis=1)
    return y * f64(c)

@@ -1,0 +1,57 @@
+import concourse.mybir as mybir
+
+BF16, F32, U16 = mybir.dt.bfloat16, mybir.dt.float32, mybir.dt.uint16
+
+P = 128
+TOKENS = 256
+FEATURES = 256
+BLOCKS = FEATURES // P
+EXPERTS = 4
+PIECE = 128
+ENTRIES = EXPERTS * PIECE
+PIECE_COLUMNS = PIECE // 16
+
+FLOPS = 2 * FEATURES * P * ENTRIES
+
+
+def tile_gather_matmul_kernel(tc, table, w, c, offs, out):
+    nc = tc.nc
+    with (
+        tc.tile_pool(name="held", bufs=1) as held,
+        tc.psum_pool(name="banks", bufs=1) as banks,
+    ):
+        offsets = held.tile([P, ENTRIES // 16], U16, name="offsets")
+        nc.sync.dma_start(offsets[:], offs)
+
+        gains = held.tile([P, ENTRIES], F32, name="gains")
+        nc.gpsimd.dma_start(gains[:], c.partition_broadcast(P))
+
+        queues = (nc.sync, nc.scalar)
+
+        windows = []
+        for b in range(BLOCKS):
+            window = held.tile([P, TOKENS], BF16, name="window%d" % b)
+            queues[b % 2].dma_start(window[:], table[b * P : (b + 1) * P, :])
+            windows.append(window)
+
+        weights = []
+        for e in range(EXPERTS):
+            matrix = held.tile([P, BLOCKS, P], BF16, name="matrix%d" % e)
+            queues[e % 2].dma_start(matrix[:], w[e].rearrange("(b p) m -> p b m", p=P))
+            weights.append(matrix)
+
+        result = held.tile([P, ENTRIES], F32, name="result")
+        for e in range(EXPERTS):
+            piece = slice(e * PIECE, (e + 1) * PIECE)
+            picked = offsets[:, e * PIECE_COLUMNS : (e + 1) * PIECE_COLUMNS]
+            bank = banks.tile([P, PIECE], F32, name="bank%d" % e)
+            for b in range(BLOCKS):
+                nc.tensor.matmul(
+                    bank[:],
+                    weights[e][:, b, :],
+                    windows[b][:].indirect(picked),
+                    start=(b == 0),
+                    stop=(b == BLOCKS - 1),
+                )
+            nc.vector.tensor_tensor(result[:, piece], bank[:], gains[:, piece], mybir.AluOpType.mult)
+            queues[e % 2].dma_start(out[:, piece], result[:, piece])

@@ -23,22 +23,17 @@ def tile_gather_matmul_kernel(tc, table, w, c, offs, out):
         offsets = held.tile([P, ENTRIES // 16], U16, name="offsets")
         nc.sync.dma_start(offsets[:], offs)
 
+        windows = [held.tile([P, TOKENS], BF16, name="window%d" % b) for b in range(BLOCKS)]
+        weights = [held.tile([P, BLOCKS, P], BF16, name="matrix%d" % e) for e in range(EXPERTS)]
         gains = held.tile([P, ENTRIES], F32, name="gains")
-        nc.gpsimd.dma_start(gains[:], c.partition_broadcast(P))
 
-        queues = (nc.sync, nc.scalar)
-
-        windows = []
-        for b in range(BLOCKS):
-            window = held.tile([P, TOKENS], BF16, name="window%d" % b)
-            queues[b % 2].dma_start(window[:], table[b * P : (b + 1) * P, :])
-            windows.append(window)
-
-        weights = []
-        for e in range(EXPERTS):
-            matrix = held.tile([P, BLOCKS, P], BF16, name="matrix%d" % e)
-            queues[e % 2].dma_start(matrix[:], w[e].rearrange("(b p) m -> p b m", p=P))
-            weights.append(matrix)
+        window_loads = [(windows[b], table[b * P : (b + 1) * P, :]) for b in range(BLOCKS)]
+        weight_loads = [(weights[e], w[e].rearrange("(b p) m -> p b m", p=P)) for e in range(EXPERTS)]
+        gains_load = (gains, c.partition_broadcast(P))
+        loads = [window_loads[0], weight_loads[0], window_loads[1], weight_loads[1], gains_load] + weight_loads[2:]
+        queues = (nc.scalar, nc.sync)
+        for i, (tile, source) in enumerate(loads):
+            queues[i % 2].dma_start(tile[:], source)
 
         result = held.tile([P, ENTRIES], F32, name="result")
         for e in range(EXPERTS):

@@ -11,6 +11,9 @@ PIECE = 128
 ENTRIES = EXPERTS * PIECE
 PIECE_COLUMNS = PIECE // 16
 
+WARM_COLUMNS = 512
+WARM_MATMULS = 4
+
 FLOPS = 2 * FEATURES * P * ENTRIES
 
 
@@ -34,6 +37,12 @@ def tile_gather_matmul_kernel(tc, table, w, c, offs, out):
         queues = (nc.scalar, nc.sync)
         for i, (tile, source) in enumerate(loads):
             queues[i % 2].dma_start(tile[:], source)
+
+        zeros = held.tile([P, WARM_COLUMNS], BF16, name="zeros")
+        nc.vector.memset(zeros[:].bitcast(F32), 0.0)
+        unread = banks.tile([P, WARM_COLUMNS], F32, name="unread")
+        for i in range(WARM_MATMULS):
+            nc.tensor.matmul(unread[:], zeros[:, 0:P], zeros[:], start=True, stop=True)
 
         result = held.tile([P, ENTRIES], F32, name="result")
         for e in range(EXPERTS):

@@ -11,9 +11,6 @@ PIECE = 128
 ENTRIES = EXPERTS * PIECE
 PIECE_COLUMNS = PIECE // 16
 
-WARM_COLUMNS = 512
-WARM_MATMULS = 4
-
 FLOPS = 2 * FEATURES * P * ENTRIES
 
 
@@ -32,17 +29,11 @@ def tile_gather_matmul_kernel(tc, table, w, c, offs, out):
 
         window_loads = [(windows[b], table[b * P : (b + 1) * P, :]) for b in range(BLOCKS)]
         weight_loads = [(weights[e], w[e].rearrange("(b p) m -> p b m", p=P)) for e in range(EXPERTS)]
-        gains_load = (gains, c.partition_broadcast(P))
-        loads = [window_loads[0], weight_loads[0], window_loads[1], weight_loads[1], gains_load] + weight_loads[2:]
+        nc.scalar.dma_start(gains[:], c.partition_broadcast(P))
+        loads = [window_loads[0], weight_loads[0], window_loads[1]] + weight_loads[1:]
+        for tile, source in loads:
+            nc.sync.dma_start(tile[:], source)
         queues = (nc.scalar, nc.sync)
-        for i, (tile, source) in enumerate(loads):
-            queues[i % 2].dma_start(tile[:], source)
-
-        zeros = held.tile([P, WARM_COLUMNS], BF16, name="zeros")
-        nc.vector.memset(zeros[:].bitcast(F32), 0.0)
-        unread = banks.tile([P, WARM_COLUMNS], F32, name="unread")
-        for i in range(WARM_MATMULS):
-            nc.tensor.matmul(unread[:], zeros[:, 0:P], zeros[:], start=True, stop=True)
 
         result = held.tile([P, ENTRIES], F32, name="result")
         for e in range(EXPERTS):

@@ -27,13 +27,14 @@ def tile_gather_matmul_kernel(tc, table, w, c, offs, out):
         weights = [held.tile([P, BLOCKS, P], BF16, name="matrix%d" % e) for e in range(EXPERTS)]
         gains = held.tile([P, ENTRIES], F32, name="gains")
 
-        window_loads = [(windows[b], table[b * P : (b + 1) * P, :]) for b in range(BLOCKS)]
-        weight_loads = [(weights[e], w[e].rearrange("(b p) m -> p b m", p=P)) for e in range(EXPERTS)]
-        nc.scalar.dma_start(gains[:], c.partition_broadcast(P))
-        loads = [window_loads[0], weight_loads[0], window_loads[1]] + weight_loads[1:]
-        for tile, source in loads:
-            nc.sync.dma_start(tile[:], source)
+        table_blocks = table.rearrange("(p b) s -> b p s", b=BLOCKS)
+        window_loads = [(windows[b], table_blocks[b]) for b in range(BLOCKS)]
+        weight_loads = [(weights[e], w[e].rearrange("(p b) m -> p b m", b=BLOCKS)) for e in range(EXPERTS)]
+        gains_load = (gains, c.partition_broadcast(P))
+        loads = [window_loads[0], weight_loads[0], window_loads[1], weight_loads[1], gains_load] + weight_loads[2:]
         queues = (nc.scalar, nc.sync)
+        for i, (tile, source) in enumerate(loads):
+            queues[i % 2].dma_start(tile[:], source)
 
         result = held.tile([P, ENTRIES], F32, name="result")
         for e in range(EXPERTS):

@@ -10,6 +10,9 @@ EXPERTS = 4
 PIECE = 128
 ENTRIES = EXPERTS * PIECE
 PIECE_COLUMNS = PIECE // 16
+SQUARE = 32
+QUADRANTS = P // SQUARE
+STRIPS = ENTRIES // SQUARE
 
 FLOPS = 2 * FEATURES * P * ENTRIES
 
@@ -25,16 +28,28 @@ def tile_gather_matmul_kernel(tc, table, w, c, offs, out):
 
         windows = [held.tile([P, TOKENS], BF16, name="window%d" % b) for b in range(BLOCKS)]
         weights = [held.tile([P, BLOCKS, P], BF16, name="matrix%d" % e) for e in range(EXPERTS)]
-        gains = held.tile([P, ENTRIES], F32, name="gains")
+        strips = held.tile([P, SQUARE], F32, name="strips", align_bytes=64)
+        nc.vector.memset(strips[:], 0.0)
+        c_strips = c.rearrange("o (t r) -> (o t) r", r=SQUARE)
+        strip_loads = [(strips[q * SQUARE : q * SQUARE + STRIPS, :], c_strips) for q in range(QUADRANTS)]
 
         table_blocks = table.rearrange("(p b) s -> b p s", b=BLOCKS)
-        window_loads = [(windows[b], table_blocks[b]) for b in range(BLOCKS)]
-        weight_loads = [(weights[e], w[e].rearrange("(p b) m -> p b m", b=BLOCKS)) for e in range(EXPERTS)]
-        gains_load = (gains, c.partition_broadcast(P))
-        loads = [window_loads[0], weight_loads[0], window_loads[1], weight_loads[1], gains_load] + weight_loads[2:]
+        window_loads = [(windows[b][:], table_blocks[b]) for b in range(BLOCKS)]
+        weight_loads = [(weights[e][:], w[e].rearrange("(p b) m -> p b m", b=BLOCKS)) for e in range(EXPERTS)]
+        loads = strip_loads + [window_loads[0], weight_loads[0], window_loads[1]] + weight_loads[1:]
         queues = (nc.scalar, nc.sync)
-        for i, (tile, source) in enumerate(loads):
-            queues[i % 2].dma_start(tile[:], source)
+        for i, (target, source) in enumerate(loads):
+            queues[i % 2].dma_start(target, source)
+
+        turned = held.tile([P, SQUARE], F32, name="turned", align_bytes=64)
+        nc.vector.transpose(turned[:], strips[:])
+        repeated = held.tile([P, ENTRIES], F32, name="repeated", align_bytes=64)
+        nc.vector.tensor_copy(
+            repeated[:].rearrange("p (t a) -> p t a", a=SQUARE),
+            turned[:, 0:STRIPS].unsqueeze(2).to_broadcast([P, STRIPS, SQUARE]),
+        )
+        gains = held.tile([P, ENTRIES], F32, name="gains", align_bytes=64)
+        nc.vector.transpose(gains[:], repeated[:])
 
         result = held.tile([P, ENTRIES], F32, name="result")
         for e in range(EXPERTS):

@@ -7,6 +7,7 @@ TOKENS = 256
 FEATURES = 256
 BLOCKS = FEATURES // P
 EXPERTS = 4
+PAIR = 2
 PIECE = 128
 ENTRIES = EXPERTS * PIECE
 PIECE_COLUMNS = PIECE // 16
@@ -27,7 +28,7 @@ def tile_gather_matmul_kernel(tc, table, w, c, offs, out):
         nc.sync.dma_start(offsets[:], offs)
 
         windows = [held.tile([P, TOKENS], BF16, name="window%d" % b) for b in range(BLOCKS)]
-        weights = [held.tile([P, BLOCKS, P], BF16, name="matrix%d" % e) for e in range(EXPERTS)]
+        weights = [held.tile([P, PAIR, BLOCKS, P], BF16, name="matrices%d" % h) for h in range(EXPERTS // PAIR)]
         strips = held.tile([P, SQUARE], F32, name="strips", align_bytes=64)
         nc.vector.memset(strips[:], 0.0)
         c_strips = c.rearrange("o (t r) -> (o t) r", r=SQUARE)
@@ -35,7 +36,10 @@ def tile_gather_matmul_kernel(tc, table, w, c, offs, out):
 
         table_blocks = table.rearrange("(p b) s -> b p s", b=BLOCKS)
         window_loads = [(windows[b][:], table_blocks[b]) for b in range(BLOCKS)]
-        weight_loads = [(weights[e][:], w[e].rearrange("(p b) m -> p b m", b=BLOCKS)) for e in range(EXPERTS)]
+        weight_loads = [
+            (weights[h][:], w[h * PAIR : (h + 1) * PAIR].rearrange("e (p b) m -> p e b m", b=BLOCKS))
+            for h in range(EXPERTS // PAIR)
+        ]
         loads = strip_loads + [window_loads[0], weight_loads[0], window_loads[1]] + weight_loads[1:]
         queues = (nc.scalar, nc.sync)
         for i, (target, source) in enumerate(loads):
@@ -59,7 +63,7 @@ def tile_gather_matmul_kernel(tc, table, w, c, offs, out):
             for b in range(BLOCKS):
                 nc.tensor.matmul(
                     bank[:],
-                    weights[e][:, b, :],
+                    weights[e // PAIR][:, e % PAIR, b, :],
                     windows[b][:].indirect(picked),
                     start=(b == 0),
                     stop=(b == BLOCKS - 1),

@@ -25,7 +25,6 @@ def tile_gather_matmul_kernel(tc, table, w, c, offs, out):
         tc.psum_pool(name="banks", bufs=1) as banks,
     ):
         offsets = held.tile([P, ENTRIES // 16], U16, name="offsets")
-        nc.sync.dma_start(offsets[:], offs)
 
         windows = [held.tile([P, TOKENS], BF16, name="window%d" % b) for b in range(BLOCKS)]
         weights = [held.tile([P, PAIR, BLOCKS, P], BF16, name="matrices%d" % h) for h in range(EXPERTS // PAIR)]
@@ -40,8 +39,11 @@ def tile_gather_matmul_kernel(tc, table, w, c, offs, out):
             (weights[h][:], w[h * PAIR : (h + 1) * PAIR].rearrange("e (p b) m -> p e b m", b=BLOCKS))
             for h in range(EXPERTS // PAIR)
         ]
-        loads = strip_loads + [window_loads[0], weight_loads[0], window_loads[1]] + weight_loads[1:]
         queues = (nc.scalar, nc.sync)
+        for i, (target, source) in enumerate(strip_loads):
+            queues[i % 2].dma_start(target, source)
+        nc.sync.dma_start(offsets[:], offs)
+        loads = [window_loads[0], weight_loads[0], window_loads[1]] + weight_loads[1:]
         for i, (target, source) in enumerate(loads):
             queues[i % 2].dma_start(target, source)
 

@@ -39,13 +39,11 @@ def tile_gather_matmul_kernel(tc, table, w, c, offs, out):
             (weights[h][:], w[h * PAIR : (h + 1) * PAIR].rearrange("e (p b) m -> p e b m", b=BLOCKS))
             for h in range(EXPERTS // PAIR)
         ]
+        list_load = (offsets[:], offs)
+        loads = strip_loads + [list_load, window_loads[0], weight_loads[0], window_loads[1]] + weight_loads[1:]
+        for target, source in loads:
+            nc.sync.dma_start(target, source)
         queues = (nc.scalar, nc.sync)
-        for i, (target, source) in enumerate(strip_loads):
-            queues[i % 2].dma_start(target, source)
-        nc.sync.dma_start(offsets[:], offs)
-        loads = [window_loads[0], weight_loads[0], window_loads[1]] + weight_loads[1:]
-        for i, (target, source) in enumerate(loads):
-            queues[i % 2].dma_start(target, source)
 
         turned = held.tile([P, SQUARE], F32, name="turned", align_bytes=64)
         nc.vector.transpose(turned[:], strips[:])

@@ -7,12 +7,10 @@ TOKENS = 256
 FEATURES = 256
 BLOCKS = FEATURES // P
 EXPERTS = 4
-PAIR = 2
 PIECE = 128
 ENTRIES = EXPERTS * PIECE
 PIECE_COLUMNS = PIECE // 16
 SQUARE = 32
-QUADRANTS = P // SQUARE
 STRIPS = ENTRIES // SQUARE
 
 FLOPS = 2 * FEATURES * P * ENTRIES
@@ -27,20 +25,19 @@ def tile_gather_matmul_kernel(tc, table, w, c, offs, out):
         offsets = held.tile([P, ENTRIES // 16], U16, name="offsets")
 
         windows = [held.tile([P, TOKENS], BF16, name="window%d" % b) for b in range(BLOCKS)]
-        weights = [held.tile([P, PAIR, BLOCKS, P], BF16, name="matrices%d" % h) for h in range(EXPERTS // PAIR)]
+        weights = [held.tile([P, BLOCKS, P], BF16, name="matrix%d" % e) for e in range(EXPERTS)]
         strips = held.tile([P, SQUARE], F32, name="strips", align_bytes=64)
-        nc.vector.memset(strips[:], 0.0)
         c_strips = c.rearrange("o (t r) -> (o t) r", r=SQUARE)
-        strip_loads = [(strips[q * SQUARE : q * SQUARE + STRIPS, :], c_strips) for q in range(QUADRANTS)]
+        strip_load = (
+            strips[:],
+            c_strips.unsqueeze(0).to_broadcast([P // STRIPS, STRIPS, SQUARE]),
+        )
 
         table_blocks = table.rearrange("(p b) s -> b p s", b=BLOCKS)
         window_loads = [(windows[b][:], table_blocks[b]) for b in range(BLOCKS)]
-        weight_loads = [
-            (weights[h][:], w[h * PAIR : (h + 1) * PAIR].rearrange("e (p b) m -> p e b m", b=BLOCKS))
-            for h in range(EXPERTS // PAIR)
-        ]
+        weight_loads = [(weights[e][:], w[e].rearrange("(p b) m -> p b m", b=BLOCKS)) for e in range(EXPERTS)]
         list_load = (offsets[:], offs)
-        loads = strip_loads + [list_load, window_loads[0], weight_loads[0], window_loads[1]] + weight_loads[1:]
+        loads = [strip_load, list_load, window_loads[0], weight_loads[0], window_loads[1]] + weight_loads[1:]
         for target, source in loads:
             nc.sync.dma_start(target, source)
         queues = (nc.scalar, nc.sync)
@@ -63,7 +60,7 @@ def tile_gather_matmul_kernel(tc, table, w, c, offs, out):
             for b in range(BLOCKS):
                 nc.tensor.matmul(
                     bank[:],
-                    weights[e // PAIR][:, e % PAIR, b, :],
+                    weights[e][:, b, :],
                     windows[b][:].indirect(picked),
                     start=(b == 0),
                     stop=(b == BLOCKS - 1),

@@ -12,6 +12,9 @@ ENTRIES = EXPERTS * PIECE
 PIECE_COLUMNS = PIECE // 16
 SQUARE = 32
 STRIPS = ENTRIES // SQUARE
+BANK = 512
+WARMERS = 4
+GROUPS = ((0, 1), (2,), (3,))
 
 FLOPS = 2 * FEATURES * P * ENTRIES
 
@@ -22,6 +25,12 @@ def tile_gather_matmul_kernel(tc, table, w, c, offs, out):
         tc.tile_pool(name="held", bufs=1) as held,
         tc.psum_pool(name="banks", bufs=1) as banks,
     ):
+        zeros = held.tile([P, BANK], BF16, name="zeros")
+        nc.vector.memset(zeros[:], 0.0)
+        unread = banks.tile([P, BANK], F32, name="unread")
+        for i in range(WARMERS):
+            nc.tensor.matmul(unread[:], zeros[:, 0:P], zeros[:], start=True, stop=True)
+
         offsets = held.tile([P, ENTRIES // 16], U16, name="offsets")
 
         windows = [held.tile([P, TOKENS], BF16, name="window%d" % b) for b in range(BLOCKS)]
@@ -40,7 +49,7 @@ def tile_gather_matmul_kernel(tc, table, w, c, offs, out):
         loads = [strip_load, list_load, window_loads[0], weight_loads[0], window_loads[1]] + weight_loads[1:]
         for target, source in loads:
             nc.sync.dma_start(target, source)
-        queues = (nc.scalar, nc.sync)
+        queues = (nc.sync, nc.scalar)
 
         turned = held.tile([P, SQUARE], F32, name="turned", align_bytes=64)
         nc.vector.transpose(turned[:], strips[:])
@@ -53,17 +62,18 @@ def tile_gather_matmul_kernel(tc, table, w, c, offs, out):
         nc.vector.transpose(gains[:], repeated[:])
 
         result = held.tile([P, ENTRIES], F32, name="result")
-        for e in range(EXPERTS):
-            piece = slice(e * PIECE, (e + 1) * PIECE)
-            picked = offsets[:, e * PIECE_COLUMNS : (e + 1) * PIECE_COLUMNS]
-            bank = banks.tile([P, PIECE], F32, name="bank%d" % e)
-            for b in range(BLOCKS):
-                nc.tensor.matmul(
-                    bank[:],
-                    weights[e][:, b, :],
-                    windows[b][:].indirect(picked),
-                    start=(b == 0),
-                    stop=(b == BLOCKS - 1),
-                )
-            nc.vector.tensor_tensor(result[:, piece], bank[:], gains[:, piece], mybir.AluOpType.mult)
-            queues[e % 2].dma_start(out[:, piece], result[:, piece])
+        for g, experts in enumerate(GROUPS):
+            bank = banks.tile([P, len(experts) * PIECE], F32, name="bank%d" % g)
+            for i, e in enumerate(experts):
+                picked = offsets[:, e * PIECE_COLUMNS : (e + 1) * PIECE_COLUMNS]
+                for b in range(BLOCKS):
+                    nc.tensor.matmul(
+                        bank[:, i * PIECE : (i + 1) * PIECE],
+                        weights[e][:, b, :],
+                        windows[b][:].indirect(picked),
+                        start=(b == 0),
+                        stop=(b == BLOCKS - 1),
+                    )
+            pieces = slice(experts[0] * PIECE, (experts[-1] + 1) * PIECE)
+            nc.vector.tensor_tensor(result[:, pieces], bank[:], gains[:, pieces], mybir.AluOpType.mult)
+            queues[g % 2].dma_start(out[:, pieces], result[:, pieces])

@@ -25,11 +25,12 @@ def tile_gather_matmul_kernel(tc, table, w, c, offs, out):
         tc.tile_pool(name="held", bufs=1) as held,
         tc.psum_pool(name="banks", bufs=1) as banks,
     ):
-        zeros = held.tile([P, BANK], BF16, name="zeros")
-        nc.vector.memset(zeros[:], 0.0)
+        zero_words = held.tile([P, BANK // 2], F32, name="zero_words")
+        nc.vector.memset(zero_words[:], 0.0)
+        zeros = zero_words[:].bitcast(BF16)
         unread = banks.tile([P, BANK], F32, name="unread")
         for i in range(WARMERS):
-            nc.tensor.matmul(unread[:], zeros[:, 0:P], zeros[:], start=True, stop=True)
+            nc.tensor.matmul(unread[:], zeros[:, 0:P], zeros, start=True, stop=True)
 
         offsets = held.tile([P, ENTRIES // 16], U16, name="offsets")
 
@@ -49,7 +50,6 @@ def tile_gather_matmul_kernel(tc, table, w, c, offs, out):
         loads = [strip_load, list_load, window_loads[0], weight_loads[0], window_loads[1]] + weight_loads[1:]
         for target, source in loads:
             nc.sync.dma_start(target, source)
-        queues = (nc.sync, nc.scalar)
 
         turned = held.tile([P, SQUARE], F32, name="turned", align_bytes=64)
         nc.vector.transpose(turned[:], strips[:])
@@ -76,4 +76,5 @@ def tile_gather_matmul_kernel(tc, table, w, c, offs, out):
                     )
             pieces = slice(experts[0] * PIECE, (experts[-1] + 1) * PIECE)
             nc.vector.tensor_tensor(result[:, pieces], bank[:], gains[:, pieces], mybir.AluOpType.mult)
-            queues[g % 2].dma_start(out[:, pieces], result[:, pieces])
+            queue = nc.sync if g == len(GROUPS) - 1 else nc.scalar
+            queue.dma_start(out[:, pieces], result[:, pieces])

import concourse.mybir as mybir

BF16, F32, U16 = mybir.dt.bfloat16, mybir.dt.float32, mybir.dt.uint16

P = 128
TOKENS = 256
FEATURES = 256
BLOCKS = FEATURES // P
EXPERTS = 4
PIECE = 128
ENTRIES = EXPERTS * PIECE
PIECE_COLUMNS = PIECE // 16
SQUARE = 32
STRIPS = ENTRIES // SQUARE
BANK = 512
WARMERS = 4
GROUPS = ((0, 1), (2,), (3,))

FLOPS = 2 * FEATURES * P * ENTRIES


def tile_gather_matmul_kernel(tc, table, w, c, offs, out):
    nc = tc.nc
    with (
        tc.tile_pool(name="held", bufs=1) as held,
        tc.psum_pool(name="banks", bufs=1) as banks,
    ):
        zero_words = held.tile([P, BANK // 2], F32, name="zero_words")
        nc.vector.memset(zero_words[:], 0.0)
        zeros = zero_words[:].bitcast(BF16)
        unread = banks.tile([P, BANK], F32, name="unread")
        for i in range(WARMERS):
            nc.tensor.matmul(unread[:], zeros[:, 0:P], zeros, start=True, stop=True)

        offsets = held.tile([P, ENTRIES // 16], U16, name="offsets")

        windows = [held.tile([P, TOKENS], BF16, name="window%d" % b) for b in range(BLOCKS)]
        weights = [held.tile([P, BLOCKS, P], BF16, name="matrix%d" % e) for e in range(EXPERTS)]
        strips = held.tile([P, SQUARE], F32, name="strips", align_bytes=64)
        c_strips = c.rearrange("o (t r) -> (o t) r", r=SQUARE)
        strip_load = (
            strips[:],
            c_strips.unsqueeze(0).to_broadcast([P // STRIPS, STRIPS, SQUARE]),
        )

        table_blocks = table.rearrange("(p b) s -> b p s", b=BLOCKS)
        window_loads = [(windows[b][:], table_blocks[b]) for b in range(BLOCKS)]
        weight_loads = [(weights[e][:], w[e].rearrange("(p b) m -> p b m", b=BLOCKS)) for e in range(EXPERTS)]
        list_load = (offsets[:], offs)
        loads = [strip_load, list_load, window_loads[0], weight_loads[0], window_loads[1]] + weight_loads[1:]
        for target, source in loads:
            nc.sync.dma_start(target, source)

        turned = held.tile([P, SQUARE], F32, name="turned", align_bytes=64)
        nc.vector.transpose(turned[:], strips[:])
        repeated = held.tile([P, ENTRIES], F32, name="repeated", align_bytes=64)
        nc.vector.tensor_copy(
            repeated[:].rearrange("p (t a) -> p t a", a=SQUARE),
            turned[:, 0:STRIPS].unsqueeze(2).to_broadcast([P, STRIPS, SQUARE]),
        )
        gains = held.tile([P, ENTRIES], F32, name="gains", align_bytes=64)
        nc.vector.transpose(gains[:], repeated[:])

        result = held.tile([P, ENTRIES], F32, name="result")
        for g, experts in enumerate(GROUPS):
            bank = banks.tile([P, len(experts) * PIECE], F32, name="bank%d" % g)
            for i, e in enumerate(experts):
                picked = offsets[:, e * PIECE_COLUMNS : (e + 1) * PIECE_COLUMNS]
                for b in range(BLOCKS):
                    nc.tensor.matmul(
                        bank[:, i * PIECE : (i + 1) * PIECE],
                        weights[e][:, b, :],
                        windows[b][:].indirect(picked),
                        start=(b == 0),
                        stop=(b == BLOCKS - 1),
                    )
            pieces = slice(experts[0] * PIECE, (experts[-1] + 1) * PIECE)
            nc.vector.tensor_tensor(result[:, pieces], bank[:], gains[:, pieces], mybir.AluOpType.mult)
            queue = nc.sync if g == len(GROUPS) - 1 else nc.scalar
            queue.dma_start(out[:, pieces], result[:, pieces])
